import numpy as np
import ml_dtypes


def mxq(x, axis, fmt="e4m3"):
    dtype, down = {"e4m3": (ml_dtypes.float8_e4m3fn, 7), "e5m2": (ml_dtypes.float8_e5m2, 14)}[fmt]
    v = np.moveaxis(np.asarray(x, np.float32).astype(ml_dtypes.bfloat16).astype(np.float64), axis, -1)
    blocks = v.reshape(v.shape[:-1] + (-1, 32))
    amax = np.abs(blocks).max(-1, keepdims=True)
    byte = np.maximum(np.where(amax > 0, np.frexp(amax)[1] - 1 + 127, 0) - down, 1)
    scale = np.exp2(byte - 127.0)
    codes = (blocks / scale).astype(np.float32).astype(dtype).astype(np.float64)
    return np.moveaxis((codes * scale).reshape(v.shape), -1, axis)


WIDE = False


def mx_kscale(k):
    if not WIDE:
        return np.ones(k)
    levels = np.array([10, -10, 5, -5, 0])
    if k % 512:
        return np.exp2(np.random.permutation(np.resize(levels, k // 32))).repeat(32)
    a = np.empty((k // 512, 16))
    for p in range(k // 512):
        a[p, :8] = np.random.permutation(np.resize(levels, 8))
        for g in range(8):
            far = levels[np.abs(levels - a[p, g]) >= 10]
            a[p, g + 8] = far[np.random.randint(len(far))]
    return np.exp2(a.ravel()).repeat(32)


BF16 = ml_dtypes.bfloat16


def bf(x):
    return np.asarray(x, np.float32).astype(BF16)


def f64(x):
    return np.asarray(x).astype(np.float64)


E2M1 = np.array([0.0, 0.5, 1.0, 1.5, 2.0, 3.0, 4.0, 6.0, -0.0, -0.5, -1.0, -1.5, -2.0, -3.0, -4.0, -6.0])


def pack_weight(w, fmt):
    k, n = w.shape
    w = f64(bf(w)).reshape(k // 32, 32, n)
    amax = np.abs(w).max(1)
    if fmt == "e4m3":
        byte = np.frexp(amax)[1] - 1 + 127 - 7
    else:
        mant, ex = np.frexp(amax / 6.0)
        byte = np.where(mant > 0.5, ex, ex - 1) + 127
    byte = np.clip(np.where(amax > 0, byte, 1), 1, 254)
    scaled = (w * np.exp2(127.0 - byte)[:, None, :]).reshape(k, n).astype(np.float32)
    by_word = np.ascontiguousarray(scaled.reshape(k // 512, 128, 4, n).transpose(0, 1, 3, 2))
    if fmt == "e4m3":
        words = by_word.astype(ml_dtypes.float8_e4m3fn).view(np.uint8)
    else:
        c = by_word.astype(ml_dtypes.float4_e2m1fn).view(np.uint8) & 0xF
        words = c[..., 0::2] | (c[..., 1::2] << 4)
    return np.ascontiguousarray(words), np.ascontiguousarray(byte.astype(np.uint8).reshape(k // 512, 16, n))


def unpack_weight(words, scales, fmt):
    g, p, n, _ = words.shape
    if fmt == "e4m3":
        vals = np.ascontiguousarray(words).view(ml_dtypes.float8_e4m3fn).astype(np.float64)
    else:
        nib = np.empty((g, p, n, 4), np.uint8)
        nib[..., 0::2] = words & 0xF
        nib[..., 1::2] = words >> 4
        vals = E2M1[nib]
    vals = vals * np.repeat(np.exp2(scales.astype(np.float64) - 127.0), 8, axis=1)[..., None]
    return vals.transpose(0, 1, 3, 2).reshape(g * 512, n)
def pack4(w):
    words, scales = pack_weight(w, "e2m1")
    return words.reshape(words.shape[0], 128, -1), scales


def unpack4(words, scales):
    return unpack_weight(words.reshape(words.shape[0], 128, -1, 2), scales, "e2m1")


S, K, M, V, N = 512, 1536, 1024, 1024, 2048


def setup_inputs():
    s = mx_kscale(K)
    u = mx_kscale(V)
    t = mx_kscale(M)
    cb = bf(np.random.standard_normal((S, K)) * s)
    binv = bf(np.random.standard_normal((K, M)) * np.sqrt(2.0 / K) / M ** 0.25 / s[:, None] * t)
    points = bf(np.random.standard_normal((N, V)) * u)
    l_words, l_scales = pack4(np.random.standard_normal((V, M)) / np.sqrt(V) / M ** 0.25 / u[:, None] / t)
    cost = bf(0.5 * np.random.standard_normal(N))
    return {"cb": cb, "binv": binv, "points": points,
            "l_words": l_words, "l_scales": l_scales, "cost": cost}


def reference(cb, binv, points, l_words, l_scales, cost):
    link = unpack4(l_words, l_scales)
    duals = np.maximum(mxq(f64(cb), 1, "e4m3") @ mxq(f64(binv), 0, "e4m3"), 0.0)
    cols = mxq(f64(points), 1, "e4m3") @ link
    r = f64(cost) - (mxq(duals, 1, "e4m3") @ mxq(cols, 1, "e4m3").T)
    return r / (1.0 + np.exp(r))

@@ -1,0 +1,333 @@
+from contextlib import ExitStack
+
+import concourse.mybir as mybir
+from concourse.masks import make_identity
+
+S, K, M, V, N = 512, 1536, 1024, 1024, 2048
+FLOPS = 2 * (S * K * M + N * V * M + S * M * N)
+
+F32 = mybir.dt.float32
+BF16 = mybir.dt.bfloat16
+I32 = mybir.dt.int32
+U32 = mybir.dt.uint32
+U8 = mybir.dt.uint8
+FP8X4 = mybir.dt.float8_e4m3fn_x4
+FP4X4 = mybir.dt.float4_e2m1fn_x4
+ACT = mybir.ActivationFunctionType
+ALU = mybir.AluOpType
+
+P = 128
+CH = 256
+NCH = N // CH
+
+
+def tile_column_pricing_s11_kernel(tc, cb, binv, points, l_words, l_scales, cost, out):
+    nc = tc.nc
+    with ExitStack() as ctx:
+        keep = ctx.enter_context(tc.tile_pool(name="keep", bufs=1))
+        flow = ctx.enter_context(tc.tile_pool(name="flow", bufs=3))
+        psum = ctx.enter_context(tc.psum_pool(name="psum", bufs=8))
+        ctx.enter_context(tc.manual_schedule())
+
+        ident = keep.tile([P, P], F32, name="ident")
+        warm = keep.tile([P, 8], F32, name="warm")
+        warm_out = keep.tile([P, 8], F32, name="warm_out")
+        lw_raw = keep.tile([P, 2, 2, 256], I32, name="lw_raw")
+        ls_raw = keep.tile([P, 2, 256], I32, name="ls_raw")
+        lw = keep.tile([P, 2, 2, 1024], U8, name="lw", align_bytes=64)
+        ls = keep.tile([P, 2, 2, 512], U8, name="ls", align_bytes=64)
+        pts_raw = [keep.tile([P, 2, V], BF16, name="pts_raw%d" % c) for c in range(NCH)]
+        cb_raw = [keep.tile([P, 2, K], BF16, name="cb_raw%d" % j) for j in range(2)]
+        binv_raw = [keep.tile([P, 4, M], BF16, name="binv_raw%d" % g) for g in range(3)]
+        cost_bc = keep.tile([P, N], BF16, name="cost_bc")
+        cb_t = keep.tile([P, 12 * 512], BF16, name="cb_t", align_bytes=64)
+        cb_q = keep.tile([P, 12 * 128], U32, name="cb_q", align_bytes=64)
+        cb_s = keep.tile([P, 12 * 128], U8, name="cb_s", align_bytes=64)
+        binv_q = keep.tile([P, 6, 512], U32, name="binv_q", align_bytes=64)
+        binv_s = keep.tile([P, 6, 512], U8, name="binv_s", align_bytes=64)
+        duals_t = keep.tile([P, 8 * 512], BF16, name="duals_t", align_bytes=64)
+        duals_q = keep.tile([P, 8 * 128], U32, name="duals_q", align_bytes=64)
+        duals_s = keep.tile([P, 8 * 128], U8, name="duals_s", align_bytes=64)
+        cols_q = [keep.tile([P, 512], U32, name="cols_q%d" % c, align_bytes=64) for c in range(NCH)]
+        cols_s = [keep.tile([P, 512], U8, name="cols_s%d" % c, align_bytes=64) for c in range(NCH)]
+        live = {}
+
+        def copy(eng, dst, src):
+            if eng == "S":
+                nc.scalar.copy(out=dst, in_=src)
+            else:
+                nc.vector.tensor_copy(out=dst, in_=src)
+
+        def quantize(codes, scales, src):
+            nc.vector.quantize_mx(out=codes.bitcast(FP8X4), scales=scales, in_=src)
+
+        def load_points(c, rts):
+            view = points[c * CH : (c + 1) * CH, :].rearrange("(r p) k -> p r k", p=P)
+            nc.sync.dma_start(out=pts_raw[c][:, rts, :], in_=view[:, rts, :])
+
+        def load_l_words(h):
+            view = l_words.bitcast(I32).rearrange("g p w -> p g w")
+            nc.sync.dma_start(out=lw_raw[:, h, :, :], in_=view[:, :, h * 256 : (h + 1) * 256])
+
+        def load_l_scales():
+            view = l_scales.bitcast(I32).rearrange("g q w -> q g w")
+            for quad in range(4):
+                nc.scalar.dma_start(out=ls_raw[32 * quad : 32 * quad + 4, :, :], in_=view[4 * quad : 4 * quad + 4, :, :])
+
+        def load_cb(j):
+            view = cb[j * 256 : (j + 1) * 256, :].rearrange("(r p) k -> p r k", p=P)
+            nc.sync.dma_start(out=cb_raw[j][:], in_=view)
+
+        def load_binv(g):
+            view = binv[g * 512 : (g + 1) * 512, :].rearrange("(p j) m -> p j m", j=4)
+            nc.sync.dma_start(out=binv_raw[g][:], in_=view)
+
+        def load_cost():
+            nc.sync.dma_start(out=cost_bc[:], in_=cost.partition_broadcast(P))
+
+        def order_l(h):
+            dst = lw[:, h, :, :].bitcast(I32).rearrange("p g (t b i) -> p g t b i", t=4, b=16)
+            src = lw_raw[:, h, :, :].rearrange("p g (b t i) -> p g t b i", b=16, t=4)
+            nc.vector.tensor_copy(out=dst, in_=src)
+            dst = ls[:, h, :, :].bitcast(I32).rearrange("p g (t b i) -> p g t b i", t=4, b=16)
+            src = ls_raw[:, :, h * 128 : (h + 1) * 128].rearrange("p g (b t i) -> p g t b i", b=16, t=4)
+            nc.vector.tensor_copy(out=dst, in_=src)
+
+        def turn(sources, dst, eng):
+            bank = psum.tile([P, 4, P], F32, name="bank", tag="bank")
+            for j, words in enumerate(sources):
+                for u in range(2):
+                    nc.tensor.transpose(bank[:, 2 * j + u, :], words[:, u:256:2], ident[:])
+            copy(eng, dst.bitcast(F32).rearrange("p (j r u) -> p j r u", j=2, u=2), bank[:].rearrange("p (j u) r -> p j r u", u=2))
+
+        def turn_points(c, rt, eng):
+            if rt == 0:
+                live["pts_t", c] = flow.tile([P, 2048], BF16, name="pts_t", tag="pts_t", align_bytes=64)
+            words = pts_raw[c][:, rt, :].bitcast(F32)
+            turn([words[:, 256 * g : 256 * (g + 1)] for g in range(2)], live["pts_t", c][:, rt * 1024 : (rt + 1) * 1024], eng)
+
+        def quant_points(c, rts=(0, 1)):
+            if rts[0] == 0:
+                live["pts_q", c] = flow.tile([P, 512], U32, name="pts_q", tag="pts_q", align_bytes=64)
+                live["pts_s", c] = flow.tile([P, 512], U8, name="pts_s", tag="pts_s", align_bytes=64)
+            a, b = rts[0], rts[-1] + 1
+            quantize(live["pts_q", c][:, a * 256 : b * 256], live["pts_s", c][:, a * 256 : b * 256], live["pts_t", c][:, a * 1024 : b * 1024])
+
+        def cols_bank(c, h, rt, eng):
+            if ("cols_t", c) not in live:
+                live["cols_t", c] = flow.tile([P, 2048], BF16, name="cols_t", tag="cols_t", align_bytes=64)
+            bank = psum.tile([P, 4, P], F32, name="bank", tag="bank")
+            for t in range(4):
+                for g in range(2):
+                    w = slice((2 * rt + g) * P, (2 * rt + g + 1) * P)
+                    nc.tensor.matmul_mx(
+                        out=bank[:, t, :],
+                        lhsT=lw[:, h, g, t * 256 : (t + 1) * 256].bitcast(FP4X4),
+                        lhsT_scale=ls[:, h, g, t * P : (t + 1) * P],
+                        rhs=live["pts_q", c][:, w].bitcast(FP8X4),
+                        rhs_scale=live["pts_s", c][:, w],
+                        start=(g == 0),
+                        stop=(g == 1),
+                    )
+            j = 2 * h + rt
+            dst = live["cols_t", c][:, j * 512 : (j + 1) * 512].rearrange("p (n t) -> p n t", t=4)
+            copy(eng, dst, bank[:].rearrange("p t n -> p n t"))
+
+        def quant_cols(c, hs=(0, 1)):
+            a, b = hs[0], hs[-1] + 1
+            quantize(cols_q[c][:, a * 256 : b * 256], cols_s[c][:, a * 256 : b * 256], live["cols_t", c][:, a * 1024 : b * 1024])
+
+        def turn_cb(j, eng):
+            sources = []
+            for q in (2 * j, 2 * j + 1):
+                st, g = divmod(q, 3)
+                sources.append(cb_raw[st // 2][:, st % 2, :].bitcast(F32)[:, 256 * g : 256 * (g + 1)])
+            turn(sources, cb_t[:, j * 1024 : (j + 1) * 1024], eng)
+
+        def quant_cb(i):
+            quantize(cb_q[:, i * 512 : (i + 1) * 512], cb_s[:, i * 512 : (i + 1) * 512], cb_t[:, i * 2048 : (i + 1) * 2048])
+
+        def order_binv(g, h, eng):
+            live["binv_t", g, h] = flow.tile([P, 2048], BF16, name="binv_t", tag="binv_t", align_bytes=64)
+            dst = live["binv_t", g, h][:].rearrange("p (t b i j) -> p t b i j", t=4, b=16, i=8)
+            src = binv_raw[g][:, :, h * 512 : (h + 1) * 512].rearrange("p j (b t i) -> p t b i j", b=16, t=4)
+            copy(eng, dst, src)
+
+        def quant_binv(g, h):
+            quantize(binv_q[:, 2 * g + h, :], binv_s[:, 2 * g + h, :], live["binv_t", g, h][:])
+
+        def duals_bank(st, h, eng):
+            bank = psum.tile([P, 4, P], F32, name="bank", tag="bank")
+            for t in range(4):
+                for g in range(3):
+                    w = slice((3 * st + g) * P, (3 * st + g + 1) * P)
+                    nc.tensor.matmul_mx(
+                        out=bank[:, t, :],
+                        lhsT=binv_q[:, 2 * g + h, t * P : (t + 1) * P].bitcast(FP8X4),
+                        lhsT_scale=binv_s[:, 2 * g + h, t * P : (t + 1) * P],
+                        rhs=cb_q[:, w].bitcast(FP8X4),
+                        rhs_scale=cb_s[:, w],
+                        start=(g == 0),
+                        stop=(g == 2),
+                    )
+            j = 2 * st + h
+            dst = duals_t[:, j * 512 : (j + 1) * 512].rearrange("p (n t) -> p n t", t=4)
+            src = bank[:].rearrange("p t n -> p n t")
+            if eng == "S":
+                nc.scalar.activation(out=dst, in_=src, func=ACT.Relu)
+            else:
+                nc.vector.tensor_scalar_max(out=dst, in0=src, scalar1=0.0)
+
+        def quant_duals(sp):
+            quantize(duals_q[:, sp * 512 : (sp + 1) * 512], duals_s[:, sp * 512 : (sp + 1) * 512], duals_t[:, sp * 2048 : (sp + 1) * 2048])
+
+        def price_bank(c, sp):
+            bank = psum.tile([P, 2, CH], F32, name="bank", tag="bank")
+            for s in range(2):
+                for h in range(2):
+                    j = 2 * (2 * sp + s) + h
+                    nc.tensor.matmul_mx(
+                        out=bank[:, s, :],
+                        lhsT=duals_q[:, j * P : (j + 1) * P].bitcast(FP8X4),
+                        lhsT_scale=duals_s[:, j * P : (j + 1) * P],
+                        rhs=cols_q[c][:, h * CH : (h + 1) * CH].bitcast(FP8X4),
+                        rhs_scale=cols_s[c][:, h * CH : (h + 1) * CH],
+                        start=(h == 0),
+                        stop=(h == 1),
+                    )
+            x = flow.tile([P, 2, CH], F32, name="x", tag="x")
+            c_bc = cost_bc[:, c * CH : (c + 1) * CH].unsqueeze(1).to_broadcast([P, 2, CH])
+            nc.vector.tensor_tensor(out=x[:], in0=bank[:], in1=c_bc, op=ALU.subtract)
+            y = flow.tile([P, 2, CH], F32, name="y", tag="y")
+            nc.scalar.activation(out=y[:], in_=x[:], func=ACT.Silu)
+            live["y", c, sp] = y
+
+        def finish(c, sp):
+            o = flow.tile([P, 2, CH], F32, name="o", tag="o", bufs=4)
+            nc.vector.tensor_scalar_mul(out=o[:], in0=live["y", c, sp][:], scalar1=-1.0)
+            view = out.rearrange("(s p) n -> p s n", p=P)
+            nc.sync.dma_start(out=view[:, 2 * sp : 2 * sp + 2, c * CH : (c + 1) * CH], in_=o[:])
+
+        nc.vector.memset(ls_raw[:], 0)
+        nc.vector.memset(warm[:], 0.0)
+        load_points(0, slice(0, 1))
+        load_points(0, slice(1, 2))
+        load_l_scales()
+        nc.scalar.activation(out=warm_out[:], in_=warm[:], func=ACT.Silu)
+        make_identity(nc, ident[:])
+        load_points(1, slice(0, 2))
+        load_l_words(0)
+        load_l_words(1)
+        load_cb(0)
+        load_binv(0)
+        load_points(2, slice(0, 2))
+        load_binv(1)
+        load_cb(1)
+        load_points(3, slice(0, 2))
+        load_binv(2)
+        load_points(4, slice(0, 2))
+        load_cost()
+        for c in range(5, NCH):
+            load_points(c, slice(0, 2))
+
+        def turn_chunk(c, engs="SS"):
+            for rt in range(2):
+                turn_points(c, rt, engs[rt])
+
+        def cols_chunk(c, engs="SSSS"):
+            for h in range(2):
+                for rt in range(2):
+                    cols_bank(c, h, rt, engs[2 * h + rt])
+
+        pending = []
+
+        def price(c, sp):
+            price_bank(c, sp)
+            if pending:
+                finish(*pending.pop(0))
+            pending.append((c, sp))
+
+        turn_chunk(0, "SV")
+        quant_points(0)
+        turn_chunk(1)
+        order_l(0)
+        order_l(1)
+        quant_points(1)
+        cols_chunk(0)
+        order_binv(0, 0, "V")
+        turn_chunk(2)
+        for j in range(2):
+            turn_cb(j, "S")
+        quant_cols(0)
+        quant_binv(0, 0)
+        order_binv(0, 1, "V")
+        quant_binv(0, 1)
+        quant_points(2)
+        quant_cb(0)
+        cols_chunk(1)
+        order_binv(1, 0, "V")
+        turn_chunk(3)
+        for j in range(2, 4):
+            turn_cb(j, "S")
+        quant_cols(1)
+        quant_binv(1, 0)
+        order_binv(1, 1, "V")
+        quant_points(3)
+        quant_binv(1, 1)
+        quant_cb(1)
+        cols_chunk(2)
+        order_binv(2, 0, "V")
+        for j in range(4, 6):
+            turn_cb(j, "S")
+        turn_chunk(4)
+        quant_binv(2, 0)
+        order_binv(2, 1, "V")
+        quant_binv(2, 1)
+        quant_cb(2)
+        cols_chunk(3)
+        quant_points(4)
+        quant_cols(2)
+        for st in range(2):
+            for h in range(2):
+                duals_bank(st, h, "VS"[h])
+        quant_cols(3)
+        quant_duals(0)
+        for st in range(2, 4):
+            for h in range(2):
+                duals_bank(st, h, "VS"[h])
+        quant_duals(1)
+        price(0, 0)
+        price(1, 0)
+        turn_chunk(5)
+        price(0, 1)
+        price(1, 1)
+        quant_points(5)
+        cols_chunk(4, "SSVS")
+        price(2, 0)
+        price(2, 1)
+        quant_cols(4)
+        turn_chunk(6)
+        price(3, 0)
+        price(3, 1)
+        quant_points(6)
+        cols_chunk(5, "SSVS")
+        price(4, 0)
+        quant_cols(5)
+        turn_chunk(7)
+        price(4, 1)
+        quant_points(7)
+        cols_chunk(6, "SSVS")
+        price(5, 0)
+        quant_cols(6)
+        price(5, 1)
+        cols_bank(7, 0, 0, "S")
+        cols_bank(7, 0, 1, "V")
+        cols_bank(7, 1, 0, "S")
+        quant_cols(7, (0,))
+        cols_bank(7, 1, 1, "S")
+        price(6, 0)
+        quant_cols(7, (1,))
+        price(6, 1)
+        price(7, 0)
+        price(7, 1)
+        finish(*pending.pop(0))

@@ -25,8 +25,7 @@ def tile_column_pricing_s11_kernel(tc, cb, binv, points, l_words, l_scales, cost
     nc = tc.nc
     with ExitStack() as ctx:
         keep = ctx.enter_context(tc.tile_pool(name="keep", bufs=1))
-        flow = ctx.enter_context(tc.tile_pool(name="flow", bufs=3))
-        psum = ctx.enter_context(tc.psum_pool(name="psum", bufs=8))
+        psum = ctx.enter_context(tc.psum_pool(name="psum", bufs=1))
         ctx.enter_context(tc.manual_schedule())
 
         ident = keep.tile([P, P], F32, name="ident")
@@ -38,7 +37,7 @@ def tile_column_pricing_s11_kernel(tc, cb, binv, points, l_words, l_scales, cost
         ls = keep.tile([P, 2, 2, 512], U8, name="ls", align_bytes=64)
         pts_raw = [keep.tile([P, 2, V], BF16, name="pts_raw%d" % c) for c in range(NCH)]
         cb_raw = [keep.tile([P, 2, K], BF16, name="cb_raw%d" % j) for j in range(2)]
-        binv_raw = [keep.tile([P, 4, M], BF16, name="binv_raw%d" % g) for g in range(3)]
+        binv_raw = [keep.tile([P, 4, 512], BF16, name="binv_raw%d" % j) for j in range(6)]
         cost_bc = keep.tile([P, N], BF16, name="cost_bc")
         cb_t = keep.tile([P, 12 * 512], BF16, name="cb_t", align_bytes=64)
         cb_q = keep.tile([P, 12 * 128], U32, name="cb_q", align_bytes=64)
@@ -51,6 +50,20 @@ def tile_column_pricing_s11_kernel(tc, cb, binv, points, l_words, l_scales, cost
         cols_q = [keep.tile([P, 512], U32, name="cols_q%d" % c, align_bytes=64) for c in range(NCH)]
         cols_s = [keep.tile([P, 512], U8, name="cols_s%d" % c, align_bytes=64) for c in range(NCH)]
         live = {}
+
+        banks = []
+        priced = []
+
+        def ring(kind, k, depth, shape, dtype):
+            if (kind, k) not in live:
+                name = "%s%d" % (kind, k % depth)
+                live[kind, k] = keep.tile(shape, dtype, name=name, tag=name, align_bytes=64)
+            return live[kind, k]
+
+        def new_bank(shape):
+            name = "bank%d" % (len(banks) % 8)
+            banks.append(psum.tile(shape, F32, name=name, tag=name))
+            return banks[-1]
 
         def copy(eng, dst, src):
             if eng == "S":
@@ -78,45 +91,63 @@ def tile_column_pricing_s11_kernel(tc, cb, binv, points, l_words, l_scales, cost
             view = cb[j * 256 : (j + 1) * 256, :].rearrange("(r p) k -> p r k", p=P)
             nc.sync.dma_start(out=cb_raw[j][:], in_=view)
 
-        def load_binv(g):
-            view = binv[g * 512 : (g + 1) * 512, :].rearrange("(p j) m -> p j m", j=4)
-            nc.sync.dma_start(out=binv_raw[g][:], in_=view)
+        def load_binv(g, h):
+            view = binv[g * 512 : (g + 1) * 512, h * 512 : (h + 1) * 512].rearrange("(p j) m -> p j m", j=4)
+            nc.sync.dma_start(out=binv_raw[2 * g + h][:], in_=view)
 
         def load_cost():
             nc.sync.dma_start(out=cost_bc[:], in_=cost.partition_broadcast(P))
 
         def order_l(h):
-            dst = lw[:, h, :, :].bitcast(I32).rearrange("p g (t b i) -> p g t b i", t=4, b=16)
-            src = lw_raw[:, h, :, :].rearrange("p g (b t i) -> p g t b i", b=16, t=4)
+            dst = lw[:, h, :, :].bitcast(I32).rearrange("p g (t c i) -> p g t c i", t=4, i=2)
+            src = lw_raw[:, h, :, :].rearrange("p g (c t i) -> p g t c i", t=4, i=2)
             nc.vector.tensor_copy(out=dst, in_=src)
-            dst = ls[:, h, :, :].bitcast(I32).rearrange("p g (t b i) -> p g t b i", t=4, b=16)
-            src = ls_raw[:, :, h * 128 : (h + 1) * 128].rearrange("p g (b t i) -> p g t b i", b=16, t=4)
+            dst = ls[:, h, :, :].bitcast(I32).rearrange("p g (t c) -> p g t c", t=4)
+            src = ls_raw[:, :, h * 128 : (h + 1) * 128].rearrange("p g (c t) -> p g t c", t=4)
             nc.vector.tensor_copy(out=dst, in_=src)
 
-        def turn(sources, dst, eng):
-            bank = psum.tile([P, 4, P], F32, name="bank", tag="bank")
-            for j, words in enumerate(sources):
+        def split(kind, k, depth, words, eng):
+            dst = ring(kind, k, depth, [P, 512], F32)
+            copy(eng, dst[:].rearrange("p (j u w) -> p j u w", j=2, u=2), words.rearrange("p (j w u) -> p j u w", j=2, u=2))
+
+        def turn(kind, k, words, dst, eng):
+            bank = new_bank([P, 4, P])
+            for j in range(2):
                 for u in range(2):
-                    nc.tensor.transpose(bank[:, 2 * j + u, :], words[:, u:256:2], ident[:])
+                    if (kind, k) in live:
+                        src = live[kind, k][:, (2 * j + u) * P : (2 * j + u + 1) * P]
+                    else:
+                        src = words[:, 256 * j + u : 256 * (j + 1) : 2]
+                    nc.tensor.transpose(bank[:, 2 * j + u, :], src, ident[:])
             copy(eng, dst.bitcast(F32).rearrange("p (j r u) -> p j r u", j=2, u=2), bank[:].rearrange("p (j u) r -> p j r u", u=2))
 
-        def turn_points(c, rt, eng):
-            if rt == 0:
-                live["pts_t", c] = flow.tile([P, 2048], BF16, name="pts_t", tag="pts_t", align_bytes=64)
-            words = pts_raw[c][:, rt, :].bitcast(F32)
-            turn([words[:, 256 * g : 256 * (g + 1)] for g in range(2)], live["pts_t", c][:, rt * 1024 : (rt + 1) * 1024], eng)
+        def points_words(c, rt):
+            return pts_raw[c][:, rt, :].bitcast(F32)
 
-        def quant_points(c, rts=(0, 1)):
-            if rts[0] == 0:
-                live["pts_q", c] = flow.tile([P, 512], U32, name="pts_q", tag="pts_q", align_bytes=64)
-                live["pts_s", c] = flow.tile([P, 512], U8, name="pts_s", tag="pts_s", align_bytes=64)
-            a, b = rts[0], rts[-1] + 1
-            quantize(live["pts_q", c][:, a * 256 : b * 256], live["pts_s", c][:, a * 256 : b * 256], live["pts_t", c][:, a * 1024 : b * 1024])
+        def cb_words(j):
+            flat = cb_raw[j // 3][:].rearrange("p r k -> p (r k)").bitcast(F32)
+            return flat[:, (j % 3) * 512 : (j % 3 + 1) * 512]
+
+        def split_points(c, rt, eng):
+            split("split_p", 2 * c + rt, 4, points_words(c, rt), eng)
+
+        def split_cb(j, eng):
+            split("split_c", j, 3, cb_words(j), eng)
+
+        def turn_points(c, rt, eng):
+            dst = ring("pts_t", c, 3, [P, 2048], BF16)
+            turn("split_p", 2 * c + rt, points_words(c, rt), dst[:, rt * 1024 : (rt + 1) * 1024], eng)
+
+        def turn_cb(j, eng):
+            turn("split_c", j, cb_words(j), cb_t[:, j * 1024 : (j + 1) * 1024], eng)
+
+        def quant_points(c, a, b):
+            codes = ring("pts_q", c, 3, [P, 512], U32)
+            scales = ring("pts_s", c, 3, [P, 512], U8)
+            quantize(codes[:, a * 256 : b * 256], scales[:, a * 256 : b * 256], live["pts_t", c][:, a * 1024 : b * 1024])
 
         def cols_bank(c, h, rt, eng):
-            if ("cols_t", c) not in live:
-                live["cols_t", c] = flow.tile([P, 2048], BF16, name="cols_t", tag="cols_t", align_bytes=64)
-            bank = psum.tile([P, 4, P], F32, name="bank", tag="bank")
+            bank = new_bank([P, 4, P])
             for t in range(4):
                 for g in range(2):
                     w = slice((2 * rt + g) * P, (2 * rt + g + 1) * P)
@@ -130,34 +161,25 @@ def tile_column_pricing_s11_kernel(tc, cb, binv, points, l_words, l_scales, cost
                         stop=(g == 1),
                     )
             j = 2 * h + rt
-            dst = live["cols_t", c][:, j * 512 : (j + 1) * 512].rearrange("p (n t) -> p n t", t=4)
+            dst = ring("cols_t", c, 3, [P, 2048], BF16)[:, j * 512 : (j + 1) * 512].rearrange("p (n t) -> p n t", t=4)
             copy(eng, dst, bank[:].rearrange("p t n -> p n t"))
 
-        def quant_cols(c, hs=(0, 1)):
-            a, b = hs[0], hs[-1] + 1
-            quantize(cols_q[c][:, a * 256 : b * 256], cols_s[c][:, a * 256 : b * 256], live["cols_t", c][:, a * 1024 : b * 1024])
-
-        def turn_cb(j, eng):
-            sources = []
-            for q in (2 * j, 2 * j + 1):
-                st, g = divmod(q, 3)
-                sources.append(cb_raw[st // 2][:, st % 2, :].bitcast(F32)[:, 256 * g : 256 * (g + 1)])
-            turn(sources, cb_t[:, j * 1024 : (j + 1) * 1024], eng)
+        def quant_cols(c, a, b):
+            quantize(cols_q[c][:, a * P : b * P], cols_s[c][:, a * P : b * P], live["cols_t", c][:, a * 512 : b * 512])
 
         def quant_cb(i):
             quantize(cb_q[:, i * 512 : (i + 1) * 512], cb_s[:, i * 512 : (i + 1) * 512], cb_t[:, i * 2048 : (i + 1) * 2048])
 
         def order_binv(g, h, eng):
-            live["binv_t", g, h] = flow.tile([P, 2048], BF16, name="binv_t", tag="binv_t", align_bytes=64)
-            dst = live["binv_t", g, h][:].rearrange("p (t b i j) -> p t b i j", t=4, b=16, i=8)
-            src = binv_raw[g][:, :, h * 512 : (h + 1) * 512].rearrange("p j (b t i) -> p t b i j", b=16, t=4)
+            dst = ring("binv_t", 3 * h + g, 3, [P, 2048], BF16)[:].rearrange("p (t c i j) -> p t c j i", t=4, i=4, j=4)
+            src = binv_raw[2 * g + h][:].rearrange("p j (c t i) -> p t c j i", t=4, i=4)
             copy(eng, dst, src)
 
         def quant_binv(g, h):
-            quantize(binv_q[:, 2 * g + h, :], binv_s[:, 2 * g + h, :], live["binv_t", g, h][:])
+            quantize(binv_q[:, 2 * g + h, :], binv_s[:, 2 * g + h, :], live["binv_t", 3 * h + g][:])
 
         def duals_bank(st, h, eng):
-            bank = psum.tile([P, 4, P], F32, name="bank", tag="bank")
+            bank = new_bank([P, 4, P])
             for t in range(4):
                 for g in range(3):
                     w = slice((3 * st + g) * P, (3 * st + g + 1) * P)
@@ -170,7 +192,7 @@ def tile_column_pricing_s11_kernel(tc, cb, binv, points, l_words, l_scales, cost
                         start=(g == 0),
                         stop=(g == 2),
                     )
-            j = 2 * st + h
+            j = 4 * (st // 2) + 2 * h + st % 2
             dst = duals_t[:, j * 512 : (j + 1) * 512].rearrange("p (n t) -> p n t", t=4)
             src = bank[:].rearrange("p t n -> p n t")
             if eng == "S":
@@ -178,36 +200,77 @@ def tile_column_pricing_s11_kernel(tc, cb, binv, points, l_words, l_scales, cost
             else:
                 nc.vector.tensor_scalar_max(out=dst, in0=src, scalar1=0.0)
 
-        def quant_duals(sp):
-            quantize(duals_q[:, sp * 512 : (sp + 1) * 512], duals_s[:, sp * 512 : (sp + 1) * 512], duals_t[:, sp * 2048 : (sp + 1) * 2048])
+        def quant_duals(sp, h):
+            j = 2 * sp + h
+            quantize(duals_q[:, j * 256 : (j + 1) * 256], duals_s[:, j * 256 : (j + 1) * 256], duals_t[:, j * 1024 : (j + 1) * 1024])
 
-        def price_bank(c, sp):
-            bank = psum.tile([P, 2, CH], F32, name="bank", tag="bank")
-            for s in range(2):
+        def piece(c, part):
+            if c < NCH - 1:
+                return 2 * part, 2, 0, CH
+            if part == 0:
+                return 0, 4, 0, P
+            return 2 * (part - 1), 2, P, P
+
+        def price_bank(c, part):
+            st0, nst, n0, width = piece(c, part)
+            bank = new_bank([P, nst, width])
+            for s in range(nst):
+                st = st0 + s
                 for h in range(2):
-                    j = 2 * (2 * sp + s) + h
+                    j = 4 * (st // 2) + 2 * h + st % 2
+                    w = slice(h * CH + n0, h * CH + n0 + width)
                     nc.tensor.matmul_mx(
                         out=bank[:, s, :],
                         lhsT=duals_q[:, j * P : (j + 1) * P].bitcast(FP8X4),
                         lhsT_scale=duals_s[:, j * P : (j + 1) * P],
-                        rhs=cols_q[c][:, h * CH : (h + 1) * CH].bitcast(FP8X4),
-                        rhs_scale=cols_s[c][:, h * CH : (h + 1) * CH],
+                        rhs=cols_q[c][:, w].bitcast(FP8X4),
+                        rhs_scale=cols_s[c][:, w],
                         start=(h == 0),
                         stop=(h == 1),
                     )
-            x = flow.tile([P, 2, CH], F32, name="x", tag="x")
-            c_bc = cost_bc[:, c * CH : (c + 1) * CH].unsqueeze(1).to_broadcast([P, 2, CH])
+            priced.append((c, part))
+            x = ring("x", len(priced) - 1, 3, [P, nst, width], F32)
+            c_bc = cost_bc[:, c * CH + n0 : c * CH + n0 + width].unsqueeze(1).to_broadcast([P, nst, width])
             nc.vector.tensor_tensor(out=x[:], in0=bank[:], in1=c_bc, op=ALU.subtract)
-            y = flow.tile([P, 2, CH], F32, name="y", tag="y")
-            nc.scalar.activation(out=y[:], in_=x[:], func=ACT.Silu)
-            live["y", c, sp] = y
 
-        def finish(c, sp):
-            o = flow.tile([P, 2, CH], F32, name="o", tag="o", bufs=4)
-            nc.vector.tensor_scalar_mul(out=o[:], in0=live["y", c, sp][:], scalar1=-1.0)
+        def soften(c, part):
+            st0, nst, n0, width = piece(c, part)
+            k = priced.index((c, part))
+            y = ring("y", k, 3, [P, nst, width], F32)
+            nc.scalar.activation(out=y[:], in_=live["x", k][:], func=ACT.Silu)
+
+        def finish(c, part, eng):
+            st0, nst, n0, width = piece(c, part)
+            k = priced.index((c, part))
+            o = ring("o", k, 4, [P, nst, width], F32)
+            if eng == "S":
+                nc.scalar.mul(out=o[:], in_=live["y", k][:], mul=-1.0)
+            else:
+                nc.vector.tensor_scalar_mul(out=o[:], in0=live["y", k][:], scalar1=-1.0)
             view = out.rearrange("(s p) n -> p s n", p=P)
-            nc.sync.dma_start(out=view[:, 2 * sp : 2 * sp + 2, c * CH : (c + 1) * CH], in_=o[:])
+            nc.sync.dma_start(out=view[:, st0 : st0 + nst, c * CH + n0 : c * CH + n0 + width], in_=o[:])
 
+        def warm_prepare():
+            src = ring("cols_t", -1, 3, [P, 512], BF16)
+            nc.vector.memset(src[:].bitcast(I32), 0x3F803F80)
+            quantize(ring("pts_q", -1, 3, [P, P], U32)[:], ring("pts_s", -1, 3, [P, P], U8)[:], src[:])
+
+        def warm_up(passes):
+            name = "bank7"
+            bank = psum.tile([P, P], F32, name=name, tag=name)
+            codes, scales = live["pts_q", -1], live["pts_s", -1]
+            for k in range(passes):
+                nc.tensor.matmul_mx(
+                    out=bank[:],
+                    lhsT=codes[:].bitcast(FP8X4),
+                    lhsT_scale=scales[:],
+                    rhs=codes[:].bitcast(FP8X4),
+                    rhs_scale=scales[:],
+                    start=True,
+                    stop=True,
+                )
+
+        warm_prepare()
         nc.vector.memset(ls_raw[:], 0)
         nc.vector.memset(warm[:], 0.0)
         load_points(0, slice(0, 1))
@@ -218,116 +281,191 @@ def tile_column_pricing_s11_kernel(tc, cb, binv, points, l_words, l_scales, cost
         load_points(1, slice(0, 2))
         load_l_words(0)
         load_l_words(1)
-        load_cb(0)
-        load_binv(0)
         load_points(2, slice(0, 2))
-        load_binv(1)
-        load_cb(1)
-        load_points(3, slice(0, 2))
-        load_binv(2)
+        load_cb(0)
+        load_binv(1, 0)
         load_points(4, slice(0, 2))
+        load_points(3, slice(0, 2))
+        load_binv(0, 0)
+        load_cb(1)
+        load_points(5, slice(0, 2))
+        load_binv(2, 0)
+        load_binv(1, 1)
+        load_binv(0, 1)
+        load_points(6, slice(0, 2))
+        load_binv(2, 1)
+        load_points(7, slice(0, 2))
         load_cost()
-        for c in range(5, NCH):
-            load_points(c, slice(0, 2))
-
-        def turn_chunk(c, engs="SS"):
-            for rt in range(2):
-                turn_points(c, rt, engs[rt])
-
-        def cols_chunk(c, engs="SSSS"):
-            for h in range(2):
-                for rt in range(2):
-                    cols_bank(c, h, rt, engs[2 * h + rt])
-
-        pending = []
-
-        def price(c, sp):
-            price_bank(c, sp)
-            if pending:
-                finish(*pending.pop(0))
-            pending.append((c, sp))
-
-        turn_chunk(0, "SV")
-        quant_points(0)
-        turn_chunk(1)
+        warm_up(12)
+        turn_points(0, 0, "V")
+        turn_points(0, 1, "S")
+        warm_up(8)
+        quant_points(0, 0, 1)
         order_l(0)
+        turn_points(1, 0, "S")
+        quant_points(0, 1, 2)
+        split_points(2, 1, "S")
+        turn_points(1, 1, "V")
         order_l(1)
-        quant_points(1)
-        cols_chunk(0)
-        order_binv(0, 0, "V")
-        turn_chunk(2)
-        for j in range(2):
-            turn_cb(j, "S")
-        quant_cols(0)
-        quant_binv(0, 0)
-        order_binv(0, 1, "V")
-        quant_binv(0, 1)
-        quant_points(2)
-        quant_cb(0)
-        cols_chunk(1)
+        split_points(2, 0, "S")
+        cols_bank(0, 0, 0, "S")
+        quant_points(1, 0, 2)
+        cols_bank(0, 0, 1, "V")
+        split_cb(0, "S")
+        cols_bank(0, 1, 0, "V")
+        split_cb(2, "V")
+        cols_bank(0, 1, 1, "S")
+        turn_points(2, 0, "S")
+        split_cb(1, "V")
+        turn_points(2, 1, "S")
+        turn_cb(0, "S")
         order_binv(1, 0, "V")
-        turn_chunk(3)
-        for j in range(2, 4):
-            turn_cb(j, "S")
-        quant_cols(1)
-        quant_binv(1, 0)
-        order_binv(1, 1, "V")
-        quant_points(3)
-        quant_binv(1, 1)
-        quant_cb(1)
-        cols_chunk(2)
+        split_points(4, 1, "V")
+        quant_cols(0, 0, 4)
+        turn_cb(1, "S")
+        turn_cb(2, "V")
+        cols_bank(1, 0, 0, "S")
+        cols_bank(1, 0, 1, "S")
+        quant_points(2, 0, 2)
+        split_points(3, 1, "S")
+        split_points(3, 0, "V")
+        cols_bank(1, 1, 0, "V")
+        split_points(4, 0, "S")
+        cols_bank(1, 1, 1, "S")
+        order_binv(0, 0, "V")
+        split_cb(4, "V")
+        split_cb(5, "V")
+        quant_binv(0, 0)
+        turn_points(3, 0, "S")
+        turn_points(3, 1, "S")
+        split_points(5, 0, "V")
+        turn_points(4, 0, "S")
+        turn_points(4, 1, "S")
+        turn_cb(3, "S")
+        quant_points(3, 0, 2)
+        quant_cb(0)
         order_binv(2, 0, "V")
-        for j in range(4, 6):
-            turn_cb(j, "S")
-        turn_chunk(4)
+        quant_binv(1, 0)
+        split_points(5, 1, "S")
+        turn_cb(4, "S")
+        turn_cb(5, "V")
         quant_binv(2, 0)
-        order_binv(2, 1, "V")
-        quant_binv(2, 1)
+        quant_cols(1, 0, 4)
+        cols_bank(2, 0, 0, "S")
+        cols_bank(2, 0, 1, "S")
+        quant_cb(1)
+        cols_bank(2, 1, 0, "S")
+        cols_bank(2, 1, 1, "V")
         quant_cb(2)
-        cols_chunk(3)
-        quant_points(4)
-        quant_cols(2)
-        for st in range(2):
-            for h in range(2):
-                duals_bank(st, h, "VS"[h])
-        quant_cols(3)
-        quant_duals(0)
-        for st in range(2, 4):
-            for h in range(2):
-                duals_bank(st, h, "VS"[h])
-        quant_duals(1)
-        price(0, 0)
-        price(1, 0)
-        turn_chunk(5)
-        price(0, 1)
-        price(1, 1)
-        quant_points(5)
-        cols_chunk(4, "SSVS")
-        price(2, 0)
-        price(2, 1)
-        quant_cols(4)
-        turn_chunk(6)
-        price(3, 0)
-        price(3, 1)
-        quant_points(6)
-        cols_chunk(5, "SSVS")
-        price(4, 0)
-        quant_cols(5)
-        turn_chunk(7)
-        price(4, 1)
-        quant_points(7)
-        cols_chunk(6, "SSVS")
-        price(5, 0)
-        quant_cols(6)
-        price(5, 1)
+        order_binv(1, 1, "S")
+        cols_bank(3, 0, 0, "V")
+        cols_bank(3, 0, 1, "S")
+        split_points(6, 0, "S")
+        cols_bank(3, 1, 0, "S")
+        quant_points(4, 0, 2)
+        cols_bank(3, 1, 1, "S")
+        turn_points(5, 0, "S")
+        turn_points(5, 1, "S")
+        duals_bank(0, 0, "S")
+        order_binv(2, 1, "V")
+        quant_binv(1, 1)
+        quant_binv(2, 1)
+        split_points(6, 1, "S")
+        split_points(7, 1, "V")
+        split_points(7, 0, "S")
+        duals_bank(1, 0, "S")
+        duals_bank(2, 0, "S")
+        order_binv(0, 1, "V")
+        duals_bank(3, 0, "S")
+        cols_bank(4, 0, 0, "V")
+        cols_bank(4, 0, 1, "S")
+        quant_binv(0, 1)
+        cols_bank(4, 1, 0, "S")
+        cols_bank(4, 1, 1, "V")
+        turn_points(6, 0, "V")
+        quant_duals(1, 0)
+        turn_points(6, 1, "V")
+        turn_points(7, 0, "S")
+        turn_points(7, 1, "S")
+        quant_duals(0, 0)
+        duals_bank(0, 1, "S")
+        quant_cols(4, 0, 4)
+        quant_points(5, 0, 2)
+        duals_bank(1, 1, "S")
+        quant_duals(0, 1)
+        duals_bank(2, 1, "S")
+        duals_bank(3, 1, "S")
+        quant_cols(2, 0, 4)
+        quant_cols(3, 0, 4)
+        price_bank(0, 0)
+        quant_duals(1, 1)
+        price_bank(1, 0)
+        cols_bank(5, 0, 0, "S")
+        soften(0, 0)
+        soften(1, 0)
+        quant_points(7, 0, 2)
+        quant_points(6, 0, 2)
+        cols_bank(5, 0, 1, "S")
+        price_bank(0, 1)
+        price_bank(1, 1)
+        finish(0, 0, "S")
+        cols_bank(5, 1, 0, "V")
+        cols_bank(5, 1, 1, "V")
+        soften(0, 1)
+        finish(0, 1, "V")
+        finish(1, 0, "S")
+        price_bank(2, 0)
+        price_bank(2, 1)
+        soften(1, 1)
+        cols_bank(6, 0, 0, "S")
+        soften(2, 0)
+        finish(1, 1, "V")
+        quant_cols(5, 0, 4)
+        cols_bank(6, 0, 1, "S")
+        price_bank(3, 0)
+        finish(2, 0, "V")
+        soften(2, 1)
+        price_bank(3, 1)
+        soften(3, 0)
+        cols_bank(6, 1, 0, "S")
+        finish(2, 1, "V")
+        finish(3, 0, "V")
+        cols_bank(6, 1, 1, "S")
+        price_bank(4, 0)
+        soften(3, 1)
+        price_bank(4, 1)
+        soften(4, 0)
+        quant_cols(6, 0, 4)
+        soften(4, 1)
+        price_bank(5, 0)
         cols_bank(7, 0, 0, "S")
-        cols_bank(7, 0, 1, "V")
+        finish(4, 0, "V")
         cols_bank(7, 1, 0, "S")
-        quant_cols(7, (0,))
+        finish(3, 1, "V")
+        soften(5, 0)
+        price_bank(5, 1)
+        finish(4, 1, "V")
+        quant_cols(7, 2, 3)
+        soften(5, 1)
+        quant_cols(7, 0, 1)
+        finish(5, 0, "V")
+        price_bank(6, 0)
+        cols_bank(7, 0, 1, "S")
         cols_bank(7, 1, 1, "S")
-        price(6, 0)
-        quant_cols(7, (1,))
-        price(6, 1)
-        price(7, 0)
-        price(7, 1)
-        finish(*pending.pop(0))
+        finish(5, 1, "V")
+        soften(6, 0)
+        quant_cols(7, 1, 2)
+        price_bank(6, 1)
+        quant_cols(7, 3, 4)
+        soften(6, 1)
+        price_bank(7, 0)
+        finish(6, 0, "V")
+        soften(7, 0)
+        price_bank(7, 1)
+        finish(6, 1, "V")
+        soften(7, 1)
+        price_bank(7, 2)
+        finish(7, 0, "V")
+        soften(7, 2)
+        finish(7, 1, "S")
+        finish(7, 2, "V")

from contextlib import ExitStack

import concourse.mybir as mybir
from concourse.masks import make_identity

S, K, M, V, N = 512, 1536, 1024, 1024, 2048
FLOPS = 2 * (S * K * M + N * V * M + S * M * N)

F32 = mybir.dt.float32
BF16 = mybir.dt.bfloat16
I32 = mybir.dt.int32
U32 = mybir.dt.uint32
U8 = mybir.dt.uint8
FP8X4 = mybir.dt.float8_e4m3fn_x4
FP4X4 = mybir.dt.float4_e2m1fn_x4
ACT = mybir.ActivationFunctionType
ALU = mybir.AluOpType

P = 128
CH = 256
NCH = N // CH


def tile_column_pricing_s11_kernel(tc, cb, binv, points, l_words, l_scales, cost, out):
    nc = tc.nc
    with ExitStack() as ctx:
        keep = ctx.enter_context(tc.tile_pool(name="keep", bufs=1))
        psum = ctx.enter_context(tc.psum_pool(name="psum", bufs=1))
        ctx.enter_context(tc.manual_schedule())

        ident = keep.tile([P, P], F32, name="ident")
        warm = keep.tile([P, 8], F32, name="warm")
        warm_out = keep.tile([P, 8], F32, name="warm_out")
        lw_raw = keep.tile([P, 2, 2, 256], I32, name="lw_raw")
        ls_raw = keep.tile([P, 2, 256], I32, name="ls_raw")
        lw = keep.tile([P, 2, 2, 1024], U8, name="lw", align_bytes=64)
        ls = keep.tile([P, 2, 2, 512], U8, name="ls", align_bytes=64)
        pts_raw = [keep.tile([P, 2, V], BF16, name="pts_raw%d" % c) for c in range(NCH)]
        cb_raw = [keep.tile([P, 2, K], BF16, name="cb_raw%d" % j) for j in range(2)]
        binv_raw = [keep.tile([P, 4, 512], BF16, name="binv_raw%d" % j) for j in range(6)]
        cost_bc = keep.tile([P, N], BF16, name="cost_bc")
        cb_t = keep.tile([P, 12 * 512], BF16, name="cb_t", align_bytes=64)
        cb_q = keep.tile([P, 12 * 128], U32, name="cb_q", align_bytes=64)
        cb_s = keep.tile([P, 12 * 128], U8, name="cb_s", align_bytes=64)
        binv_q = keep.tile([P, 6, 512], U32, name="binv_q", align_bytes=64)
        binv_s = keep.tile([P, 6, 512], U8, name="binv_s", align_bytes=64)
        duals_t = keep.tile([P, 8 * 512], BF16, name="duals_t", align_bytes=64)
        duals_q = keep.tile([P, 8 * 128], U32, name="duals_q", align_bytes=64)
        duals_s = keep.tile([P, 8 * 128], U8, name="duals_s", align_bytes=64)
        cols_q = [keep.tile([P, 512], U32, name="cols_q%d" % c, align_bytes=64) for c in range(NCH)]
        cols_s = [keep.tile([P, 512], U8, name="cols_s%d" % c, align_bytes=64) for c in range(NCH)]
        live = {}

        banks = []
        priced = []

        def ring(kind, k, depth, shape, dtype):
            if (kind, k) not in live:
                name = "%s%d" % (kind, k % depth)
                live[kind, k] = keep.tile(shape, dtype, name=name, tag=name, align_bytes=64)
            return live[kind, k]

        def new_bank(shape):
            name = "bank%d" % (len(banks) % 8)
            banks.append(psum.tile(shape, F32, name=name, tag=name))
            return banks[-1]

        def copy(eng, dst, src):
            if eng == "S":
                nc.scalar.copy(out=dst, in_=src)
            else:
                nc.vector.tensor_copy(out=dst, in_=src)

        def quantize(codes, scales, src):
            nc.vector.quantize_mx(out=codes.bitcast(FP8X4), scales=scales, in_=src)

        def load_points(c, rts):
            view = points[c * CH : (c + 1) * CH, :].rearrange("(r p) k -> p r k", p=P)
            nc.sync.dma_start(out=pts_raw[c][:, rts, :], in_=view[:, rts, :])

        def load_l_words(h):
            view = l_words.bitcast(I32).rearrange("g p w -> p g w")
            nc.sync.dma_start(out=lw_raw[:, h, :, :], in_=view[:, :, h * 256 : (h + 1) * 256])

        def load_l_scales():
            view = l_scales.bitcast(I32).rearrange("g q w -> q g w")
            for quad in range(4):
                nc.scalar.dma_start(out=ls_raw[32 * quad : 32 * quad + 4, :, :], in_=view[4 * quad : 4 * quad + 4, :, :])

        def load_cb(j):
            view = cb[j * 256 : (j + 1) * 256, :].rearrange("(r p) k -> p r k", p=P)
            nc.sync.dma_start(out=cb_raw[j][:], in_=view)

        def load_binv(g, h):
            view = binv[g * 512 : (g + 1) * 512, h * 512 : (h + 1) * 512].rearrange("(p j) m -> p j m", j=4)
            nc.sync.dma_start(out=binv_raw[2 * g + h][:], in_=view)

        def load_cost():
            nc.sync.dma_start(out=cost_bc[:], in_=cost.partition_broadcast(P))

        def order_l(h):
            dst = lw[:, h, :, :].bitcast(I32).rearrange("p g (t c i) -> p g t c i", t=4, i=2)
            src = lw_raw[:, h, :, :].rearrange("p g (c t i) -> p g t c i", t=4, i=2)
            nc.vector.tensor_copy(out=dst, in_=src)
            dst = ls[:, h, :, :].bitcast(I32).rearrange("p g (t c) -> p g t c", t=4)
            src = ls_raw[:, :, h * 128 : (h + 1) * 128].rearrange("p g (c t) -> p g t c", t=4)
            nc.vector.tensor_copy(out=dst, in_=src)

        def split(kind, k, depth, words, eng):
            dst = ring(kind, k, depth, [P, 512], F32)
            copy(eng, dst[:].rearrange("p (j u w) -> p j u w", j=2, u=2), words.rearrange("p (j w u) -> p j u w", j=2, u=2))

        def turn(kind, k, words, dst, eng):
            bank = new_bank([P, 4, P])
            for j in range(2):
                for u in range(2):
                    if (kind, k) in live:
                        src = live[kind, k][:, (2 * j + u) * P : (2 * j + u + 1) * P]
                    else:
                        src = words[:, 256 * j + u : 256 * (j + 1) : 2]
                    nc.tensor.transpose(bank[:, 2 * j + u, :], src, ident[:])
            copy(eng, dst.bitcast(F32).rearrange("p (j r u) -> p j r u", j=2, u=2), bank[:].rearrange("p (j u) r -> p j r u", u=2))

        def points_words(c, rt):
            return pts_raw[c][:, rt, :].bitcast(F32)

        def cb_words(j):
            flat = cb_raw[j // 3][:].rearrange("p r k -> p (r k)").bitcast(F32)
            return flat[:, (j % 3) * 512 : (j % 3 + 1) * 512]

        def split_points(c, rt, eng):
            split("split_p", 2 * c + rt, 4, points_words(c, rt), eng)

        def split_cb(j, eng):
            split("split_c", j, 3, cb_words(j), eng)

        def turn_points(c, rt, eng):
            dst = ring("pts_t", c, 3, [P, 2048], BF16)
            turn("split_p", 2 * c + rt, points_words(c, rt), dst[:, rt * 1024 : (rt + 1) * 1024], eng)

        def turn_cb(j, eng):
            turn("split_c", j, cb_words(j), cb_t[:, j * 1024 : (j + 1) * 1024], eng)

        def quant_points(c, a, b):
            codes = ring("pts_q", c, 3, [P, 512], U32)
            scales = ring("pts_s", c, 3, [P, 512], U8)
            quantize(codes[:, a * 256 : b * 256], scales[:, a * 256 : b * 256], live["pts_t", c][:, a * 1024 : b * 1024])

        def cols_bank(c, h, rt, eng):
            bank = new_bank([P, 4, P])
            for t in range(4):
                for g in range(2):
                    w = slice((2 * rt + g) * P, (2 * rt + g + 1) * P)
                    nc.tensor.matmul_mx(
                        out=bank[:, t, :],
                        lhsT=lw[:, h, g, t * 256 : (t + 1) * 256].bitcast(FP4X4),
                        lhsT_scale=ls[:, h, g, t * P : (t + 1) * P],
                        rhs=live["pts_q", c][:, w].bitcast(FP8X4),
                        rhs_scale=live["pts_s", c][:, w],
                        start=(g == 0),
                        stop=(g == 1),
                    )
            j = 2 * h + rt
            dst = ring("cols_t", c, 3, [P, 2048], BF16)[:, j * 512 : (j + 1) * 512].rearrange("p (n t) -> p n t", t=4)
            copy(eng, dst, bank[:].rearrange("p t n -> p n t"))

        def quant_cols(c, a, b):
            quantize(cols_q[c][:, a * P : b * P], cols_s[c][:, a * P : b * P], live["cols_t", c][:, a * 512 : b * 512])

        def quant_cb(i):
            quantize(cb_q[:, i * 512 : (i + 1) * 512], cb_s[:, i * 512 : (i + 1) * 512], cb_t[:, i * 2048 : (i + 1) * 2048])

        def order_binv(g, h, eng):
            dst = ring("binv_t", 3 * h + g, 3, [P, 2048], BF16)[:].rearrange("p (t c i j) -> p t c j i", t=4, i=4, j=4)
            src = binv_raw[2 * g + h][:].rearrange("p j (c t i) -> p t c j i", t=4, i=4)
            copy(eng, dst, src)

        def quant_binv(g, h):
            quantize(binv_q[:, 2 * g + h, :], binv_s[:, 2 * g + h, :], live["binv_t", 3 * h + g][:])

        def duals_bank(st, h, eng):
            bank = new_bank([P, 4, P])
            for t in range(4):
                for g in range(3):
                    w = slice((3 * st + g) * P, (3 * st + g + 1) * P)
                    nc.tensor.matmul_mx(
                        out=bank[:, t, :],
                        lhsT=binv_q[:, 2 * g + h, t * P : (t + 1) * P].bitcast(FP8X4),
                        lhsT_scale=binv_s[:, 2 * g + h, t * P : (t + 1) * P],
                        rhs=cb_q[:, w].bitcast(FP8X4),
                        rhs_scale=cb_s[:, w],
                        start=(g == 0),
                        stop=(g == 2),
                    )
            j = 4 * (st // 2) + 2 * h + st % 2
            dst = duals_t[:, j * 512 : (j + 1) * 512].rearrange("p (n t) -> p n t", t=4)
            src = bank[:].rearrange("p t n -> p n t")
            if eng == "S":
                nc.scalar.activation(out=dst, in_=src, func=ACT.Relu)
            else:
                nc.vector.tensor_scalar_max(out=dst, in0=src, scalar1=0.0)

        def quant_duals(sp, h):
            j = 2 * sp + h
            quantize(duals_q[:, j * 256 : (j + 1) * 256], duals_s[:, j * 256 : (j + 1) * 256], duals_t[:, j * 1024 : (j + 1) * 1024])

        def piece(c, part):
            if c < NCH - 1:
                return 2 * part, 2, 0, CH
            if part == 0:
                return 0, 4, 0, P
            return 2 * (part - 1), 2, P, P

        def price_bank(c, part):
            st0, nst, n0, width = piece(c, part)
            bank = new_bank([P, nst, width])
            for s in range(nst):
                st = st0 + s
                for h in range(2):
                    j = 4 * (st // 2) + 2 * h + st % 2
                    w = slice(h * CH + n0, h * CH + n0 + width)
                    nc.tensor.matmul_mx(
                        out=bank[:, s, :],
                        lhsT=duals_q[:, j * P : (j + 1) * P].bitcast(FP8X4),
                        lhsT_scale=duals_s[:, j * P : (j + 1) * P],
                        rhs=cols_q[c][:, w].bitcast(FP8X4),
                        rhs_scale=cols_s[c][:, w],
                        start=(h == 0),
                        stop=(h == 1),
                    )
            priced.append((c, part))
            x = ring("x", len(priced) - 1, 3, [P, nst, width], F32)
            c_bc = cost_bc[:, c * CH + n0 : c * CH + n0 + width].unsqueeze(1).to_broadcast([P, nst, width])
            nc.vector.tensor_tensor(out=x[:], in0=bank[:], in1=c_bc, op=ALU.subtract)

        def soften(c, part):
            st0, nst, n0, width = piece(c, part)
            k = priced.index((c, part))
            y = ring("y", k, 3, [P, nst, width], F32)
            nc.scalar.activation(out=y[:], in_=live["x", k][:], func=ACT.Silu)

        def finish(c, part, eng):
            st0, nst, n0, width = piece(c, part)
            k = priced.index((c, part))
            o = ring("o", k, 4, [P, nst, width], F32)
            if eng == "S":
                nc.scalar.mul(out=o[:], in_=live["y", k][:], mul=-1.0)
            else:
                nc.vector.tensor_scalar_mul(out=o[:], in0=live["y", k][:], scalar1=-1.0)
            view = out.rearrange("(s p) n -> p s n", p=P)
            nc.sync.dma_start(out=view[:, st0 : st0 + nst, c * CH + n0 : c * CH + n0 + width], in_=o[:])

        def warm_prepare():
            src = ring("cols_t", -1, 3, [P, 512], BF16)
            nc.vector.memset(src[:].bitcast(I32), 0x3F803F80)
            quantize(ring("pts_q", -1, 3, [P, P], U32)[:], ring("pts_s", -1, 3, [P, P], U8)[:], src[:])

        def warm_up(passes):
            name = "bank7"
            bank = psum.tile([P, P], F32, name=name, tag=name)
            codes, scales = live["pts_q", -1], live["pts_s", -1]
            for k in range(passes):
                nc.tensor.matmul_mx(
                    out=bank[:],
                    lhsT=codes[:].bitcast(FP8X4),
                    lhsT_scale=scales[:],
                    rhs=codes[:].bitcast(FP8X4),
                    rhs_scale=scales[:],
                    start=True,
                    stop=True,
                )

        warm_prepare()
        nc.vector.memset(ls_raw[:], 0)
        nc.vector.memset(warm[:], 0.0)
        load_points(0, slice(0, 1))
        load_points(0, slice(1, 2))
        load_l_scales()
        nc.scalar.activation(out=warm_out[:], in_=warm[:], func=ACT.Silu)
        make_identity(nc, ident[:])
        load_points(1, slice(0, 2))
        load_l_words(0)
        load_l_words(1)
        load_points(2, slice(0, 2))
        load_cb(0)
        load_binv(1, 0)
        load_points(4, slice(0, 2))
        load_points(3, slice(0, 2))
        load_binv(0, 0)
        load_cb(1)
        load_points(5, slice(0, 2))
        load_binv(2, 0)
        load_binv(1, 1)
        load_binv(0, 1)
        load_points(6, slice(0, 2))
        load_binv(2, 1)
        load_points(7, slice(0, 2))
        load_cost()
        warm_up(12)
        turn_points(0, 0, "V")
        turn_points(0, 1, "S")
        warm_up(8)
        quant_points(0, 0, 1)
        order_l(0)
        turn_points(1, 0, "S")
        quant_points(0, 1, 2)
        split_points(2, 1, "S")
        turn_points(1, 1, "V")
        order_l(1)
        split_points(2, 0, "S")
        cols_bank(0, 0, 0, "S")
        quant_points(1, 0, 2)
        cols_bank(0, 0, 1, "V")
        split_cb(0, "S")
        cols_bank(0, 1, 0, "V")
        split_cb(2, "V")
        cols_bank(0, 1, 1, "S")
        turn_points(2, 0, "S")
        split_cb(1, "V")
        turn_points(2, 1, "S")
        turn_cb(0, "S")
        order_binv(1, 0, "V")
        split_points(4, 1, "V")
        quant_cols(0, 0, 4)
        turn_cb(1, "S")
        turn_cb(2, "V")
        cols_bank(1, 0, 0, "S")
        cols_bank(1, 0, 1, "S")
        quant_points(2, 0, 2)
        split_points(3, 1, "S")
        split_points(3, 0, "V")
        cols_bank(1, 1, 0, "V")
        split_points(4, 0, "S")
        cols_bank(1, 1, 1, "S")
        order_binv(0, 0, "V")
        split_cb(4, "V")
        split_cb(5, "V")
        quant_binv(0, 0)
        turn_points(3, 0, "S")
        turn_points(3, 1, "S")
        split_points(5, 0, "V")
        turn_points(4, 0, "S")
        turn_points(4, 1, "S")
        turn_cb(3, "S")
        quant_points(3, 0, 2)
        quant_cb(0)
        order_binv(2, 0, "V")
        quant_binv(1, 0)
        split_points(5, 1, "S")
        turn_cb(4, "S")
        turn_cb(5, "V")
        quant_binv(2, 0)
        quant_cols(1, 0, 4)
        cols_bank(2, 0, 0, "S")
        cols_bank(2, 0, 1, "S")
        quant_cb(1)
        cols_bank(2, 1, 0, "S")
        cols_bank(2, 1, 1, "V")
        quant_cb(2)
        order_binv(1, 1, "S")
        cols_bank(3, 0, 0, "V")
        cols_bank(3, 0, 1, "S")
        split_points(6, 0, "S")
        cols_bank(3, 1, 0, "S")
        quant_points(4, 0, 2)
        cols_bank(3, 1, 1, "S")
        turn_points(5, 0, "S")
        turn_points(5, 1, "S")
        duals_bank(0, 0, "S")
        order_binv(2, 1, "V")
        quant_binv(1, 1)
        quant_binv(2, 1)
        split_points(6, 1, "S")
        split_points(7, 1, "V")
        split_points(7, 0, "S")
        duals_bank(1, 0, "S")
        duals_bank(2, 0, "S")
        order_binv(0, 1, "V")
        duals_bank(3, 0, "S")
        cols_bank(4, 0, 0, "V")
        cols_bank(4, 0, 1, "S")
        quant_binv(0, 1)
        cols_bank(4, 1, 0, "S")
        cols_bank(4, 1, 1, "V")
        turn_points(6, 0, "V")
        quant_duals(1, 0)
        turn_points(6, 1, "V")
        turn_points(7, 0, "S")
        turn_points(7, 1, "S")
        quant_duals(0, 0)
        duals_bank(0, 1, "S")
        quant_cols(4, 0, 4)
        quant_points(5, 0, 2)
        duals_bank(1, 1, "S")
        quant_duals(0, 1)
        duals_bank(2, 1, "S")
        duals_bank(3, 1, "S")
        quant_cols(2, 0, 4)
        quant_cols(3, 0, 4)
        price_bank(0, 0)
        quant_duals(1, 1)
        price_bank(1, 0)
        cols_bank(5, 0, 0, "S")
        soften(0, 0)
        soften(1, 0)
        quant_points(7, 0, 2)
        quant_points(6, 0, 2)
        cols_bank(5, 0, 1, "S")
        price_bank(0, 1)
        price_bank(1, 1)
        finish(0, 0, "S")
        cols_bank(5, 1, 0, "V")
        cols_bank(5, 1, 1, "V")
        soften(0, 1)
        finish(0, 1, "V")
        finish(1, 0, "S")
        price_bank(2, 0)
        price_bank(2, 1)
        soften(1, 1)
        cols_bank(6, 0, 0, "S")
        soften(2, 0)
        finish(1, 1, "V")
        quant_cols(5, 0, 4)
        cols_bank(6, 0, 1, "S")
        price_bank(3, 0)
        finish(2, 0, "V")
        soften(2, 1)
        price_bank(3, 1)
        soften(3, 0)
        cols_bank(6, 1, 0, "S")
        finish(2, 1, "V")
        finish(3, 0, "V")
        cols_bank(6, 1, 1, "S")
        price_bank(4, 0)
        soften(3, 1)
        price_bank(4, 1)
        soften(4, 0)
        quant_cols(6, 0, 4)
        soften(4, 1)
        price_bank(5, 0)
        cols_bank(7, 0, 0, "S")
        finish(4, 0, "V")
        cols_bank(7, 1, 0, "S")
        finish(3, 1, "V")
        soften(5, 0)
        price_bank(5, 1)
        finish(4, 1, "V")
        quant_cols(7, 2, 3)
        soften(5, 1)
        quant_cols(7, 0, 1)
        finish(5, 0, "V")
        price_bank(6, 0)
        cols_bank(7, 0, 1, "S")
        cols_bank(7, 1, 1, "S")
        finish(5, 1, "V")
        soften(6, 0)
        quant_cols(7, 1, 2)
        price_bank(6, 1)
        quant_cols(7, 3, 4)
        soften(6, 1)
        price_bank(7, 0)
        finish(6, 0, "V")
        soften(7, 0)
        price_bank(7, 1)
        finish(6, 1, "V")
        soften(7, 1)
        price_bank(7, 2)
        finish(7, 0, "V")
        soften(7, 2)
        finish(7, 1, "S")
        finish(7, 2, "V")
